import numpy as np, ml_dtypes
CORES = [3,5,19,21,35,37,51,53,67,69]
N = 10
import mx_ref
BF = ml_dtypes.bfloat16
def gentries(a):
    return np.ascontiguousarray(a.reshape(8, 16, -1).transpose(0, 2, 1)).reshape(8, -1)
def gtable(e):
    e = np.asarray(e); return np.ascontiguousarray(e.reshape(8, -1, 16).transpose(0, 2, 1)).reshape(128, -1).astype(np.int32)
def gcols(t, e):
    v = np.concatenate([t.reshape(8, 16, -1, 4), np.zeros((8, 16, 1, 4), BF)], axis=2)
    return np.ascontiguousarray(np.stack([v[g][:, e[g]] for g in range(8)])).reshape(128, -1)
def f(rng, *shape):
    return mx_ref.flush((rng.standard_normal(shape, dtype=np.float32) * np.exp2(rng.integers(-2, 3, shape[:-1] + (1,)))).astype(BF))
def wide(rng, *shape, cols=0):
    v = rng.standard_normal(shape, dtype=np.float32) * np.exp2(rng.integers(-12, 13, shape)).astype(np.float32)
    if cols: v *= np.repeat(np.exp2(rng.integers(-cols, cols + 1, shape[:-2] + (1, shape[-1] // 4))) * (rng.random(shape[:-2] + (1, shape[-1] // 4)) > 0.0625), 4, axis=-1).astype(np.float32)
    return mx_ref.flush(v.astype(BF))
S = 128
def block(rng, how):
    if how == "one": return np.full((8, S), rng.integers(0, 128))
    if how == "groups": return np.tile(rng.integers(0, 128, S), (8, 1))
    if how == "ends": return np.stack([rng.permutation(np.arange(S) % 2 * 127) for g in range(8)])
    if how == "distinct": return np.stack([np.tile(rng.permutation(128), S // 128) for g in range(8)])
    return rng.integers(0, 128, (8, S))
def lists(rng, how=""):
    return {"cw": np.stack([gtable(np.concatenate([block(rng, how) for s in range(N)], axis=1)) for r in range(N)])}
def setup_inputs(rng):
    return {"bk": f(rng, N, 128, 512), "x": f(rng, N, 128, 512 * N), **lists(rng)}
def setup_inputs_one(rng):
    return {**setup_inputs(rng), **lists(rng, "one")}
def setup_inputs_groups(rng):
    return {**setup_inputs(rng), **lists(rng, "groups")}
def setup_inputs_ends(rng):
    return {**setup_inputs(rng), **lists(rng, "ends")}
def setup_inputs_distinct(rng):
    return {**setup_inputs(rng), **lists(rng, "distinct")}
def setup_inputs_spread(rng):
    d = setup_inputs(rng); d["bk"] = wide(rng, N, 128, 512, cols=4); d["x"] = wide(rng, N, 128, 512 * N); return d
def check_inputs(d):
    b = []
    for r in range(N):
        e = d["cw"][r]
        if e.min() < 0 or e.max() > 127: b.append("cw")
    return b
def reference(bk, x, cw):
    y = np.zeros((N, 128, S), np.float32)
    for r in range(N):
        e = gentries(cw[r])
        for s in range(N):
            W = gcols(bk[s], e[:, S * s:S * s + S])
            X = np.ascontiguousarray(x[r][:, 512 * s:512 * s + 512])
            y[r] += mx_ref.matmul(mx_ref.quantize(X), mx_ref.quantize(W))
    return {"y": y}

from concourse.bass import DstId, RemoteDMATransfer
from concourse.mybir import dt, ActivationFunctionType

N = 10
S = 128
K = S // 16
PAIR = 2
STEPS = N // PAIR - 1
MATE, OWN = N - 2, N - 1
SPLIT = 192
XA = 5

SCRATCH = {
    "cwi": ("sbuf", [128, N * K], "int32"),
    "cwu": ("sbuf", [128, N * K], "uint16"),
    "lst": ("sbuf", [128, (N - 1) * K + K], "uint16"),
    "book": ("sbuf", [128, 4 * S], "bfloat16"),
    "win": ("sbuf", [128, 4 * S], "bfloat16"),
    "h": ("sbuf", [128, 4 * S * N], "bfloat16"),
    "wq": ("sbuf", [128, S * N], "float8_e4m3fn_x4"),
    "ws": ("sbuf", [128, S * N], "uint8"),
    "xb": ("sbuf", [128, 4 * S * N], "bfloat16"),
    "xq": ("sbuf", [128, S * N], "float8_e4m3fn_x4"),
    "xs": ("sbuf", [128, S * N], "uint8"),
    "rq": ("sbuf", [128, S * (N - 1)], "float8_e4m3fn_x4"),
    "rs": ("sbuf", [128, S * (N - 1)], "uint8"),
    "acc": ("psum", [128, 512], "float32"),
    "yb": ("sbuf", [128, S], "float32"),
}
BATCHES = ["m%d" % m for m in range(1, STEPS + 1)] + ["mate"]
SEMAPHORES = (["ldcw", "ldbk", "ldxa", "ldxb", "conv", "winv", "wins", "lsent", "wsent", "xqd", "prod", "ycp", "stored"]
              + ["list_" + b for b in BATCHES] + ["land_" + b for b in BATCHES]
              + ["gath_" + b for b in BATCHES + ["own"]] + ["quan_" + b for b in BATCHES + ["own"]])


def bits(engines):
    return sum(1 << e for e in engines)


def rank_program(g, core, T, topo):
    rank = T.rank_of(core)
    if rank is None:
        return
    sem = T.sem
    cores = list(T.cores)
    chips = []
    for c in cores:
        if topo.chip(c) not in chips:
            chips.append(topo.chip(c))
    homes = [[r for r in range(N) if topo.chip(cores[r]) == ch] for ch in chips]
    q = chips.index(topo.chip(core))
    me = homes[q].index(rank)
    mate = homes[q][1 - me]
    nch = len(chips)

    def send(dst_rank, engines, remote_sem, src, dst):
        rid, pid, _ = topo.addr(cores[dst_rank])
        return RemoteDMATransfer(dst_ids=[DstId(rid=rid, pnc=pid)], dma_engine_mask=bits(engines),
                                 remote_sem=remote_sem, src=src, dst=dst)

    def share(dst_ranks):
        es = topo.engines(core, cores[dst_ranks[0]])
        n = len(es) // len(dst_ranks)
        return [es[i * n:(i + 1) * n] for i in range(len(dst_ranks))]

    far = topo.engines(core, cores[homes[(q + 1) % nch][0]])
    near = [e for e in topo.engines(core, cores[mate]) if e not in far]

    def to_step(m):
        return homes[(q + m) % nch]

    def from_step(m):
        return homes[(q - m) % nch]

    g.sync.dma_start(T.cwi[:], T.cw[:]).then_inc(sem.ldcw, 16)
    g.scalar.dma_start(T.book[:], T.bk[:]).then_inc(sem.ldbk, 16)
    cut = 4 * S * XA
    g.sync.dma_start(T.xb[:, 0:cut], T.x[:, 0:cut]).then_inc(sem.ldxa, 16)

    lsent = 0
    wsent = 0
    g.wait_ge(sem.conv, 1)
    for m in range(1, STEPS + 1):
        at = PAIR * K * (m - 1) + K * me
        tr = []
        for s, es in zip(from_step(m), share(from_step(m))):
            tr.append(send(s, es, sem["list_m%d" % m], T.cwu[:, K * s:K * s + K], T.lst[:, at:at + K]))
            lsent += len(es)
        g.remote_dma_fused(tr, local_sem=sem.lsent)
    g.remote_dma_fused([send(mate, near, sem.list_mate, T.cwu[:, K * mate:K * mate + K], T.lst[:, K * MATE:K * MATE + K])],
                       local_sem=sem.lsent)
    lsent += len(near)

    def codes(src_slot, slot, r, es, remote_sem):
        return send(r, es, remote_sem, T.wq[:, S * src_slot:S * src_slot + S].bitcast(dt.uint8),
                    T.rq[:, S * slot:S * slot + S].bitcast(dt.uint8))

    def scales(src_slot, slot, r, es, remote_sem):
        return send(r, es, remote_sem, T.ws[:, S * src_slot:S * src_slot + S], T.rs[:, S * slot:S * slot + S])

    def far_call(make, ms):
        ranks = [(m, i, r) for m in ms for i, r in enumerate(to_step(m))]
        tr = []
        n = 0
        for (m, i, r), es in zip(ranks, share([r for _, _, r in ranks])):
            base = PAIR * (m - 1)
            tr.append(make(base + i, base + me, r, es, sem["land_m%d" % m]))
            n += len(es)
        g.remote_dma_fused(tr, local_sem=sem.wsent)
        return n

    landed = {}
    for m in range(1, STEPS + 1):
        g.wait_ge(sem["quan_m%d" % m], 1)
        if m % 2:
            wsent += far_call(codes, [m])
        elif m < STEPS:
            wsent += far_call(codes, [m])
            wsent += far_call(scales, [m - 1, m])
        else:
            wsent += far_call(scales, [m - 1, m])
            wsent += far_call(codes, [m])
        landed[m] = PAIR * (len(far) // PAIR + len(far) // (2 * PAIR))
    g.wait_ge(sem.quan_mate, 1)
    g.remote_dma_fused([codes(MATE, MATE, mate, near, sem.land_mate)], local_sem=sem.wsent)
    g.remote_dma_fused([scales(MATE, MATE, mate, near, sem.land_mate)], local_sem=sem.wsent)
    wsent += 2 * len(near)

    g.sync.wait_ge(sem.lsent, lsent)
    g.sync.dma_start(T.xb[:, cut:], T.x[:, cut:]).then_inc(sem.ldxb, 16)

    def offs(buf, at, lo, hi):
        return buf[:, at + lo // 16:at + hi // 16]

    def vgather(t, slot, buf, at, lo, hi, done):
        a, b = S * slot + lo, S * slot + hi
        g.vector.tensor_copy(T.h[:, 4 * a + t:4 * b:4],
                             T.win[:, S * t:S * t + S].indirect(offs(buf, at, lo, hi))).then_inc(done, 1)

    def sgather(t, slot, buf, at, lo, hi, done):
        a, b = S * slot + lo, S * slot + hi
        g.scalar.activation(T.h[:, 4 * a + t:4 * b:4],
                            T.win[:, S * t:S * t + S].indirect(offs(buf, at, lo, hi)),
                            ActivationFunctionType.Copy).then_inc(done, 1)

    def quant(slot, n, done):
        a, b = S * slot, S * (slot + n)
        g.vector.quantize_mx(T.wq[:, a:b], T.ws[:, a:b], T.h[:, 4 * a:4 * b]).then_inc(done, 1)

    g.vector.wait_ge(sem.ldcw, 16)
    g.vector.tensor_copy(T.cwu[:], T.cwi[:]).then_inc(sem.conv, 1)
    g.vector.wait_ge(sem.ldbk, 16)
    for t in (0, 1):
        g.vector.tensor_copy(T.win[:, S * t:S * t + S], T.book[:, t:4 * S:4]).then_inc(sem.winv, 1)
    g.vector.wait_ge(sem.winv, 2)
    g.vector.wait_ge(sem.conv, 1)
    g.scalar.wait_ge(sem.ldbk, 16)
    for t in (2, 3):
        g.scalar.activation(T.win[:, S * t:S * t + S], T.book[:, t:4 * S:4], ActivationFunctionType.Copy).then_inc(sem.wins, 1)
    g.scalar.wait_ge(sem.wins, 2)
    g.scalar.wait_ge(sem.winv, 2)
    g.scalar.wait_ge(sem.conv, 1)

    own = sem.gath_own
    for t in (0, 1):
        vgather(t, OWN, T.cwu, K * rank, 0, S, own)
    for t in (2, 3):
        sgather(t, OWN, T.cwu, K * rank, 0, S, own)
    g.vector.wait_ge(own, 4)
    quant(OWN, 1, sem.quan_own)

    for m in range(1, STEPS + 1):
        slot, at = PAIR * (m - 1), PAIR * K * (m - 1)
        arrived, want = sem["list_m%d" % m], PAIR * (len(far) // PAIR)
        done = sem["gath_m%d" % m]
        g.vector.wait_ge(arrived, want)
        vgather(0, slot, T.lst, at, 0, PAIR * S, done)
        vgather(1, slot, T.lst, at, 0, SPLIT, done)
        g.scalar.wait_ge(arrived, want)
        sgather(2, slot, T.lst, at, 0, PAIR * S, done)
        sgather(3, slot, T.lst, at, 0, PAIR * S, done)
        sgather(1, slot, T.lst, at, SPLIT, PAIR * S, done)
        g.vector.wait_ge(done, 5)
        quant(slot, PAIR, sem["quan_m%d" % m])

    done = sem.gath_mate
    g.vector.wait_ge(sem.list_mate, len(near))
    g.scalar.wait_ge(sem.list_mate, len(near))
    for t in (0, 1):
        vgather(t, MATE, T.lst, K * MATE, 0, S, done)
    for t in (2, 3):
        sgather(t, MATE, T.lst, K * MATE, 0, S, done)
    g.vector.wait_ge(done, 4)
    quant(MATE, 1, sem.quan_mate)

    nx = 0
    for ready, lo, hi in ((sem.ldxa, 0, S * XA), (sem.ldxb, S * XA, S * N)):
        g.vector.wait_ge(ready, 16)
        while lo < hi:
            b = min(hi, lo + 4 * S)
            g.vector.quantize_mx(T.xq[:, lo:b], T.xs[:, lo:b], T.xb[:, 4 * lo:4 * b]).then_inc(sem.xqd, 1)
            nx += 1
            lo = b

    def product(s, wq, ws, slot, start=False, stop=False):
        i = g.tensor.matmul_mx(T.acc[:, 0:S], T.xq[:, S * s:S * s + S], T.xs[:, S * s:S * s + S],
                               wq[:, S * slot:S * slot + S], ws[:, S * slot:S * slot + S], start, stop)
        if stop:
            i.then_inc(sem.prod, 1)

    g.tensor.wait_ge(sem.xqd, nx)
    g.tensor.wait_ge(sem.quan_own, 1)
    product(rank, T.wq, T.ws, OWN, start=True)
    for m in range(1, STEPS + 1):
        if m == STEPS:
            g.tensor.wait_ge(sem.land_mate, 2 * len(near))
            product(mate, T.rq, T.rs, MATE)
        g.tensor.wait_ge(sem["land_m%d" % m], landed[m])
        for i, s in enumerate(from_step(m)):
            product(s, T.rq, T.rs, PAIR * (m - 1) + i, stop=m == STEPS and i == PAIR - 1)

    g.vector.wait_ge(sem.prod, 1)
    g.vector.tensor_copy(T.yb[:], T.acc[:, 0:S]).then_inc(sem.ycp, 1)
    g.sync.wait_ge(sem.ycp, 1)
    g.sync.dma_start(T.y[:], T.yb[:]).then_inc(sem.stored, 16)
    g.sync.wait_ge(sem.stored, 16)

    g.wait_ge(sem.lsent, lsent)
    g.wait_ge(sem.wsent, wsent)
